import numpy as np
import ml_dtypes

BF16 = ml_dtypes.bfloat16


def bf(x):
    return np.asarray(x, np.float32).astype(BF16)


def f32(x):
    return np.asarray(x, np.float32)


def f64(x):
    return np.asarray(x).astype(np.float64)


def striped(idx):
    return np.tile(idx.reshape(-1, 16).T, (8, 1))


S, K, M, N, D, V = 512, 128, 512, 384, 3, 128


def setup_inputs():
    return {"table": bf(np.random.standard_normal((K, S))), "w": bf(np.random.standard_normal((D, K, M)) / np.sqrt(D * K)), "b": f32(0.5 * np.random.standard_normal((M, 1))), "offs": striped(np.random.permutation(np.tile(np.arange(S), 2))[:N])}


def reference(table, w, b, offs):
    idx = offs[:16].T.reshape(-1)
    x = f64(table)[:, idx]
    y = sum(f64(w)[t].T @ x[:, t * V : (t + 1) * V] for t in range(D))
    return np.maximum(y + f64(b), 0.0)

@@ -1,0 +1,50 @@
+import concourse.mybir as mybir
+
+BF16, F32, U16 = mybir.dt.bfloat16, mybir.dt.float32, mybir.dt.uint16
+RELU = mybir.ActivationFunctionType.Relu
+ADD, MAX = mybir.AluOpType.add, mybir.AluOpType.max
+
+P = 128
+NODES = 512
+RELATIONS = 3
+PICKED = 128
+M = 512
+M_BLOCKS = M // P
+PIECE_COLS = PICKED // 16
+
+FLOPS = 2 * M * PICKED * RELATIONS * P
+
+
+def tile_gather_matmul_kernel(tc, table, w, b, offs, out):
+    nc = tc.nc
+    with tc.tile_pool(name="held", bufs=1) as held, tc.psum_pool(name="banks", bufs=1) as banks:
+        offsets = held.tile([P, RELATIONS * PIECE_COLS], U16, name="offsets")
+        nc.sync.dma_start(offsets[:], offs)
+        nodes = held.tile([P, NODES], BF16, name="nodes")
+        nc.scalar.dma_start(nodes[:], table)
+        weights = [held.tile([P, M], BF16, name="weights%d" % t) for t in range(RELATIONS)]
+        nc.sync.dma_start(weights[0][:], w[0])
+        nc.scalar.dma_start(weights[1][:], w[1])
+        nc.sync.dma_start(weights[2][:], w[2])
+        bias = held.tile([P, M_BLOCKS], F32, name="bias")
+        with nc.allow_non_contiguous_dma(reason="512 single float32 values, one to a partition and block"):
+            nc.gpsimd.dma_start(bias[:], b.rearrange("(a p) o -> p (a o)", p=P))
+
+        result = held.tile([P, M_BLOCKS, PICKED], F32, name="result")
+        for a in range(M_BLOCKS):
+            bank = banks.tile([P, PICKED], F32, name="bank%d" % a)
+            for t in range(RELATIONS):
+                picked = nodes[:].indirect(offsets[:, t * PIECE_COLS : (t + 1) * PIECE_COLS])
+                nc.tensor.matmul(
+                    bank[:],
+                    weights[t][:, a * P : (a + 1) * P],
+                    picked,
+                    start=(t == 0),
+                    stop=(t == RELATIONS - 1),
+                )
+            if a % 2 == 0:
+                nc.scalar.activation(result[:, a, :], bank[:], RELU, bias=bias[:, a : a + 1])
+                nc.sync.dma_start(out[a * P : (a + 1) * P, :], result[:, a, :])
+            else:
+                nc.vector.tensor_scalar(result[:, a, :], bank[:], bias[:, a : a + 1], 0.0, op0=ADD, op1=MAX)
+                nc.scalar.dma_start(out[a * P : (a + 1) * P, :], result[:, a, :])

@@ -12,6 +12,9 @@ M = 512
 M_BLOCKS = M // P
 PIECE_COLS = PICKED // 16
 
+BANK_COLS = 512
+WARMING_MATMULS = 6
+
 FLOPS = 2 * M * PICKED * RELATIONS * P
 
 
@@ -29,6 +32,12 @@ def tile_gather_matmul_kernel(tc, table, w, b, offs, out):
         bias = held.tile([P, M_BLOCKS], F32, name="bias")
         with nc.allow_non_contiguous_dma(reason="512 single float32 values, one to a partition and block"):
             nc.gpsimd.dma_start(bias[:], b.rearrange("(a p) o -> p (a o)", p=P))
+
+        zeros = held.tile([P, BANK_COLS], BF16, name="zeros")
+        nc.vector.memset(zeros[:], 0.0)
+        unread = banks.tile([P, BANK_COLS], F32, name="unread")
+        for i in range(WARMING_MATMULS):
+            nc.tensor.matmul(unread[:], zeros[:, 0:P], zeros[:], start=True, stop=True)
 
         result = held.tile([P, M_BLOCKS, PICKED], F32, name="result")
         for a in range(M_BLOCKS):

@@ -1,7 +1,6 @@
 import concourse.mybir as mybir
 
 BF16, F32, U16 = mybir.dt.bfloat16, mybir.dt.float32, mybir.dt.uint16
-RELU = mybir.ActivationFunctionType.Relu
 ADD, MAX = mybir.AluOpType.add, mybir.AluOpType.max
 
 P = 128
@@ -31,7 +30,7 @@ def tile_gather_matmul_kernel(tc, table, w, b, offs, out):
         nc.sync.dma_start(weights[2][:], w[2])
         bias = held.tile([P, M_BLOCKS], F32, name="bias")
         with nc.allow_non_contiguous_dma(reason="512 single float32 values, one to a partition and block"):
-            nc.gpsimd.dma_start(bias[:], b.rearrange("(a p) o -> p (a o)", p=P))
+            nc.scalar.dma_start(bias[:], b.rearrange("(a p) o -> p (a o)", p=P))
 
         zeros = held.tile([P, BANK_COLS], BF16, name="zeros")
         nc.vector.memset(zeros[:], 0.0)
@@ -39,21 +38,20 @@ def tile_gather_matmul_kernel(tc, table, w, b, offs, out):
         for i in range(WARMING_MATMULS):
             nc.tensor.matmul(unread[:], zeros[:, 0:P], zeros[:], start=True, stop=True)
 
-        result = held.tile([P, M_BLOCKS, PICKED], F32, name="result")
-        for a in range(M_BLOCKS):
-            bank = banks.tile([P, PICKED], F32, name="bank%d" % a)
-            for t in range(RELATIONS):
-                picked = nodes[:].indirect(offsets[:, t * PIECE_COLS : (t + 1) * PIECE_COLS])
+        bank = [banks.tile([P, PICKED], F32, name="bank%d" % a) for a in range(M_BLOCKS)]
+        for t in range(RELATIONS):
+            picked = nodes[:].indirect(offsets[:, t * PIECE_COLS : (t + 1) * PIECE_COLS])
+            for a in range(M_BLOCKS):
                 nc.tensor.matmul(
-                    bank[:],
+                    bank[a][:],
                     weights[t][:, a * P : (a + 1) * P],
                     picked,
                     start=(t == 0),
                     stop=(t == RELATIONS - 1),
                 )
-            if a % 2 == 0:
-                nc.scalar.activation(result[:, a, :], bank[:], RELU, bias=bias[:, a : a + 1])
-                nc.sync.dma_start(out[a * P : (a + 1) * P, :], result[:, a, :])
-            else:
-                nc.vector.tensor_scalar(result[:, a, :], bank[:], bias[:, a : a + 1], 0.0, op0=ADD, op1=MAX)
-                nc.scalar.dma_start(out[a * P : (a + 1) * P, :], result[:, a, :])
+
+        result = held.tile([P, M_BLOCKS, PICKED], F32, name="result")
+        for a in range(M_BLOCKS):
+            nc.vector.tensor_scalar(result[:, a, :], bank[a][:], bias[:, a : a + 1], 0.0, op0=ADD, op1=MAX)
+            store_queue = nc.sync if a % 2 == 0 else nc.scalar
+            store_queue.dma_start(out[a * P : (a + 1) * P, :], result[:, a, :])

@@ -12,7 +12,7 @@ M_BLOCKS = M // P
 PIECE_COLS = PICKED // 16
 
 BANK_COLS = 512
-WARMING_MATMULS = 6
+WARMING_MATMULS = 3
 
 FLOPS = 2 * M * PICKED * RELATIONS * P
 
@@ -39,19 +39,23 @@ def tile_gather_matmul_kernel(tc, table, w, b, offs, out):
             nc.tensor.matmul(unread[:], zeros[:, 0:P], zeros[:], start=True, stop=True)
 
         bank = [banks.tile([P, PICKED], F32, name="bank%d" % a) for a in range(M_BLOCKS)]
-        for t in range(RELATIONS):
-            picked = nodes[:].indirect(offsets[:, t * PIECE_COLS : (t + 1) * PIECE_COLS])
-            for a in range(M_BLOCKS):
-                nc.tensor.matmul(
-                    bank[a][:],
-                    weights[t][:, a * P : (a + 1) * P],
-                    picked,
-                    start=(t == 0),
-                    stop=(t == RELATIONS - 1),
-                )
+
+        def add_relation(a, t):
+            nc.tensor.matmul(
+                bank[a][:],
+                weights[t][:, a * P : (a + 1) * P],
+                nodes[:].indirect(offsets[:, t * PIECE_COLS : (t + 1) * PIECE_COLS]),
+                start=(t == 0),
+                stop=(t == RELATIONS - 1),
+            )
+
+        for a in range(M_BLOCKS):
+            add_relation(a, 0)
 
         result = held.tile([P, M_BLOCKS, PICKED], F32, name="result")
         for a in range(M_BLOCKS):
+            for t in range(1, RELATIONS):
+                add_relation(a, t)
             nc.vector.tensor_scalar(result[:, a, :], bank[a][:], bias[:, a : a + 1], 0.0, op0=ADD, op1=MAX)
             store_queue = nc.sync if a % 2 == 0 else nc.scalar
             store_queue.dma_start(out[a * P : (a + 1) * P, :], result[:, a, :])

@@ -12,7 +12,7 @@ M_BLOCKS = M // P
 PIECE_COLS = PICKED // 16
 
 BANK_COLS = 512
-WARMING_MATMULS = 3
+WARMING_MATMULS = 4
 
 FLOPS = 2 * M * PICKED * RELATIONS * P
 

@@ -20,17 +20,27 @@ FLOPS = 2 * M * PICKED * RELATIONS * P
 def tile_gather_matmul_kernel(tc, table, w, b, offs, out):
     nc = tc.nc
     with tc.tile_pool(name="held", bufs=1) as held, tc.psum_pool(name="banks", bufs=1) as banks:
-        offsets = held.tile([P, RELATIONS * PIECE_COLS], U16, name="offsets")
-        nc.sync.dma_start(offsets[:], offs)
         nodes = held.tile([P, NODES], BF16, name="nodes")
         nc.scalar.dma_start(nodes[:], table)
-        weights = [held.tile([P, M], BF16, name="weights%d" % t) for t in range(RELATIONS)]
-        nc.sync.dma_start(weights[0][:], w[0])
-        nc.scalar.dma_start(weights[1][:], w[1])
-        nc.sync.dma_start(weights[2][:], w[2])
+        offsets = held.tile([P, RELATIONS * PIECE_COLS], U16, name="offsets")
+        nc.sync.dma_start(offsets[:], offs)
+        first_weights = held.tile([P, P], BF16, name="first_weights")
+        nc.sync.dma_start(first_weights[:], w[0][:, 0:P])
+        other_weights0 = held.tile([P, M - P], BF16, name="other_weights0")
+        nc.sync.dma_start(other_weights0[:], w[0][:, P:M])
+        weights1 = held.tile([P, M], BF16, name="weights1")
+        nc.sync.dma_start(weights1[:], w[1])
+        weights2 = held.tile([P, M], BF16, name="weights2")
+        nc.sync.dma_start(weights2[:], w[2])
         bias = held.tile([P, M_BLOCKS], F32, name="bias")
         with nc.allow_non_contiguous_dma(reason="512 single float32 values, one to a partition and block"):
-            nc.scalar.dma_start(bias[:], b.rearrange("(a p) o -> p (a o)", p=P))
+            nc.sync.dma_start(bias[:], b.rearrange("(a p) o -> p (a o)", p=P))
+
+        weight_block = [
+            [first_weights[:]] + [other_weights0[:, (a - 1) * P : a * P] for a in range(1, M_BLOCKS)],
+            [weights1[:, a * P : (a + 1) * P] for a in range(M_BLOCKS)],
+            [weights2[:, a * P : (a + 1) * P] for a in range(M_BLOCKS)],
+        ]
 
         zeros = held.tile([P, BANK_COLS], BF16, name="zeros")
         nc.vector.memset(zeros[:], 0.0)
@@ -43,7 +53,7 @@ def tile_gather_matmul_kernel(tc, table, w, b, offs, out):
         def add_relation(a, t):
             nc.tensor.matmul(
                 bank[a][:],
-                weights[t][:, a * P : (a + 1) * P],
+                weight_block[t][a],
                 nodes[:].indirect(offsets[:, t * PIECE_COLS : (t + 1) * PIECE_COLS]),
                 start=(t == 0),
                 stop=(t == RELATIONS - 1),

@@ -11,9 +11,6 @@ M = 512
 M_BLOCKS = M // P
 PIECE_COLS = PICKED // 16
 
-BANK_COLS = 512
-WARMING_MATMULS = 4
-
 FLOPS = 2 * M * PICKED * RELATIONS * P
 
 
@@ -41,12 +38,6 @@ def tile_gather_matmul_kernel(tc, table, w, b, offs, out):
             [weights1[:, a * P : (a + 1) * P] for a in range(M_BLOCKS)],
             [weights2[:, a * P : (a + 1) * P] for a in range(M_BLOCKS)],
         ]
-
-        zeros = held.tile([P, BANK_COLS], BF16, name="zeros")
-        nc.vector.memset(zeros[:], 0.0)
-        unread = banks.tile([P, BANK_COLS], F32, name="unread")
-        for i in range(WARMING_MATMULS):
-            nc.tensor.matmul(unread[:], zeros[:, 0:P], zeros[:], start=True, stop=True)
 
         bank = [banks.tile([P, PICKED], F32, name="bank%d" % a) for a in range(M_BLOCKS)]
 

@@ -18,7 +18,7 @@ def tile_gather_matmul_kernel(tc, table, w, b, offs, out):
     nc = tc.nc
     with tc.tile_pool(name="held", bufs=1) as held, tc.psum_pool(name="banks", bufs=1) as banks:
         nodes = held.tile([P, NODES], BF16, name="nodes")
-        nc.scalar.dma_start(nodes[:], table)
+        nc.sync.dma_start(nodes[:], table)
         offsets = held.tile([P, RELATIONS * PIECE_COLS], U16, name="offsets")
         nc.sync.dma_start(offsets[:], offs)
         first_weights = held.tile([P, P], BF16, name="first_weights")

@@ -21,30 +21,19 @@ def tile_gather_matmul_kernel(tc, table, w, b, offs, out):
         nc.sync.dma_start(nodes[:], table)
         offsets = held.tile([P, RELATIONS * PIECE_COLS], U16, name="offsets")
         nc.sync.dma_start(offsets[:], offs)
-        first_weights = held.tile([P, P], BF16, name="first_weights")
-        nc.sync.dma_start(first_weights[:], w[0][:, 0:P])
-        other_weights0 = held.tile([P, M - P], BF16, name="other_weights0")
-        nc.sync.dma_start(other_weights0[:], w[0][:, P:M])
-        weights1 = held.tile([P, M], BF16, name="weights1")
-        nc.sync.dma_start(weights1[:], w[1])
-        weights2 = held.tile([P, M], BF16, name="weights2")
-        nc.sync.dma_start(weights2[:], w[2])
+        weights = [held.tile([P, M], BF16, name="weights%d" % t) for t in range(RELATIONS)]
+        for t in range(RELATIONS):
+            nc.sync.dma_start(weights[t][:], w[t])
         bias = held.tile([P, M_BLOCKS], F32, name="bias")
         with nc.allow_non_contiguous_dma(reason="512 single float32 values, one to a partition and block"):
             nc.sync.dma_start(bias[:], b.rearrange("(a p) o -> p (a o)", p=P))
-
-        weight_block = [
-            [first_weights[:]] + [other_weights0[:, (a - 1) * P : a * P] for a in range(1, M_BLOCKS)],
-            [weights1[:, a * P : (a + 1) * P] for a in range(M_BLOCKS)],
-            [weights2[:, a * P : (a + 1) * P] for a in range(M_BLOCKS)],
-        ]
 
         bank = [banks.tile([P, PICKED], F32, name="bank%d" % a) for a in range(M_BLOCKS)]
 
         def add_relation(a, t):
             nc.tensor.matmul(
                 bank[a][:],
-                weight_block[t][a],
+                weights[t][:, a * P : (a + 1) * P],
                 nodes[:].indirect(offsets[:, t * PIECE_COLS : (t + 1) * PIECE_COLS]),
                 start=(t == 0),
                 stop=(t == RELATIONS - 1),

@@ -21,9 +21,15 @@ def tile_gather_matmul_kernel(tc, table, w, b, offs, out):
         nc.sync.dma_start(nodes[:], table)
         offsets = held.tile([P, RELATIONS * PIECE_COLS], U16, name="offsets")
         nc.sync.dma_start(offsets[:], offs)
-        weights = [held.tile([P, M], BF16, name="weights%d" % t) for t in range(RELATIONS)]
-        for t in range(RELATIONS):
-            nc.sync.dma_start(weights[t][:], w[t])
+        first_weights = held.tile([P, M], BF16, name="first_weights")
+        nc.sync.dma_start(first_weights[:], w[0])
+        later_weights = held.tile([P, RELATIONS - 1, M], BF16, name="later_weights")
+        nc.sync.dma_start(later_weights[:], w[1:RELATIONS].rearrange("t k m -> k t m"))
+
+        def weights(t, a):
+            columns = slice(a * P, (a + 1) * P)
+            return first_weights[:, columns] if t == 0 else later_weights[:, t - 1, columns]
+
         bias = held.tile([P, M_BLOCKS], F32, name="bias")
         with nc.allow_non_contiguous_dma(reason="512 single float32 values, one to a partition and block"):
             nc.sync.dma_start(bias[:], b.rearrange("(a p) o -> p (a o)", p=P))
@@ -33,7 +39,7 @@ def tile_gather_matmul_kernel(tc, table, w, b, offs, out):
         def add_relation(a, t):
             nc.tensor.matmul(
                 bank[a][:],
-                weights[t][:, a * P : (a + 1) * P],
+                weights(t, a),
                 nodes[:].indirect(offsets[:, t * PIECE_COLS : (t + 1) * PIECE_COLS]),
                 start=(t == 0),
                 stop=(t == RELATIONS - 1),
@@ -47,5 +53,8 @@ def tile_gather_matmul_kernel(tc, table, w, b, offs, out):
             for t in range(1, RELATIONS):
                 add_relation(a, t)
             nc.vector.tensor_scalar(result[:, a, :], bank[a][:], bias[:, a : a + 1], 0.0, op0=ADD, op1=MAX)
-            store_queue = nc.sync if a % 2 == 0 else nc.scalar
-            store_queue.dma_start(out[a * P : (a + 1) * P, :], result[:, a, :])
+            if a == 1:
+                nc.scalar.dma_start(out[0 : 2 * P, :].rearrange("(a p) v -> p a v", p=P), result[:, 0:2, :])
+            elif a >= 2:
+                store_queue = nc.sync if a % 2 == 0 else nc.scalar
+                store_queue.dma_start(out[a * P : (a + 1) * P, :], result[:, a, :])

@@ -9,6 +9,7 @@ RELATIONS = 3
 PICKED = 128
 M = 512
 M_BLOCKS = M // P
+ROW_ALIGN = 256
 PIECE_COLS = PICKED // 16
 
 FLOPS = 2 * M * PICKED * RELATIONS * P
@@ -17,13 +18,13 @@ FLOPS = 2 * M * PICKED * RELATIONS * P
 def tile_gather_matmul_kernel(tc, table, w, b, offs, out):
     nc = tc.nc
     with tc.tile_pool(name="held", bufs=1) as held, tc.psum_pool(name="banks", bufs=1) as banks:
-        nodes = held.tile([P, NODES], BF16, name="nodes")
+        nodes = held.tile([P, NODES], BF16, name="nodes", align_bytes=ROW_ALIGN)
         nc.sync.dma_start(nodes[:], table)
         offsets = held.tile([P, RELATIONS * PIECE_COLS], U16, name="offsets")
         nc.sync.dma_start(offsets[:], offs)
-        first_weights = held.tile([P, M], BF16, name="first_weights")
+        first_weights = held.tile([P, M], BF16, name="first_weights", align_bytes=ROW_ALIGN)
         nc.sync.dma_start(first_weights[:], w[0])
-        later_weights = held.tile([P, RELATIONS - 1, M], BF16, name="later_weights")
+        later_weights = held.tile([P, RELATIONS - 1, M], BF16, name="later_weights", align_bytes=ROW_ALIGN)
         nc.sync.dma_start(later_weights[:], w[1:RELATIONS].rearrange("t k m -> k t m"))
 
         def weights(t, a):
@@ -48,7 +49,7 @@ def tile_gather_matmul_kernel(tc, table, w, b, offs, out):
         for a in range(M_BLOCKS):
             add_relation(a, 0)
 
-        result = held.tile([P, M_BLOCKS, PICKED], F32, name="result")
+        result = held.tile([P, M_BLOCKS, PICKED], F32, name="result", align_bytes=ROW_ALIGN)
         for a in range(M_BLOCKS):
             for t in range(1, RELATIONS):
                 add_relation(a, t)

import concourse.mybir as mybir

BF16, F32, U16 = mybir.dt.bfloat16, mybir.dt.float32, mybir.dt.uint16
ADD, MAX = mybir.AluOpType.add, mybir.AluOpType.max

P = 128
NODES = 512
RELATIONS = 3
PICKED = 128
M = 512
M_BLOCKS = M // P
ROW_ALIGN = 256
PIECE_COLS = PICKED // 16

FLOPS = 2 * M * PICKED * RELATIONS * P


def tile_gather_matmul_kernel(tc, table, w, b, offs, out):
    nc = tc.nc
    with tc.tile_pool(name="held", bufs=1) as held, tc.psum_pool(name="banks", bufs=1) as banks:
        nodes = held.tile([P, NODES], BF16, name="nodes", align_bytes=ROW_ALIGN)
        nc.sync.dma_start(nodes[:], table)
        offsets = held.tile([P, RELATIONS * PIECE_COLS], U16, name="offsets")
        nc.sync.dma_start(offsets[:], offs)
        first_weights = held.tile([P, M], BF16, name="first_weights", align_bytes=ROW_ALIGN)
        nc.sync.dma_start(first_weights[:], w[0])
        later_weights = held.tile([P, RELATIONS - 1, M], BF16, name="later_weights", align_bytes=ROW_ALIGN)
        nc.sync.dma_start(later_weights[:], w[1:RELATIONS].rearrange("t k m -> k t m"))

        def weights(t, a):
            columns = slice(a * P, (a + 1) * P)
            return first_weights[:, columns] if t == 0 else later_weights[:, t - 1, columns]

        bias = held.tile([P, M_BLOCKS], F32, name="bias")
        with nc.allow_non_contiguous_dma(reason="512 single float32 values, one to a partition and block"):
            nc.sync.dma_start(bias[:], b.rearrange("(a p) o -> p (a o)", p=P))

        bank = [banks.tile([P, PICKED], F32, name="bank%d" % a) for a in range(M_BLOCKS)]

        def add_relation(a, t):
            nc.tensor.matmul(
                bank[a][:],
                weights(t, a),
                nodes[:].indirect(offsets[:, t * PIECE_COLS : (t + 1) * PIECE_COLS]),
                start=(t == 0),
                stop=(t == RELATIONS - 1),
            )

        for a in range(M_BLOCKS):
            add_relation(a, 0)

        result = held.tile([P, M_BLOCKS, PICKED], F32, name="result", align_bytes=ROW_ALIGN)
        for a in range(M_BLOCKS):
            for t in range(1, RELATIONS):
                add_relation(a, t)
            nc.vector.tensor_scalar(result[:, a, :], bank[a][:], bias[:, a : a + 1], 0.0, op0=ADD, op1=MAX)
            if a == 1:
                nc.scalar.dma_start(out[0 : 2 * P, :].rearrange("(a p) v -> p a v", p=P), result[:, 0:2, :])
            elif a >= 2:
                store_queue = nc.sync if a % 2 == 0 else nc.scalar
                store_queue.dma_start(out[a * P : (a + 1) * P, :], result[:, a, :])
